import numpy as np, ml_dtypes
CORES = [24,48,72,152,176,200]
N = 6
import mx_ref
NC, KT, ROOT = 128, 1, 0
BF = ml_dtypes.bfloat16
def setup_inputs(rng):
    def f(*shape):
        return mx_ref.flush((rng.standard_normal(shape, dtype=np.float32) * np.exp2(rng.integers(-2, 3, shape[:-1] + (1,)))).astype(BF))
    return {"w": f(N, 128, KT * 512), "x": f(N, 128, N * KT * 4 * NC)}
def setup_inputs_blocks(rng):
    d = setup_inputs(rng)
    for k in ("w", "x"): d[k] = mx_ref.spread(d[k], rng, 4)
    return d
def setup_inputs_wide(rng):
    d = setup_inputs(rng)
    for k in ("w", "x"): d[k] = mx_ref.flush((d[k].astype(np.float32) * np.exp2(rng.integers(-8, 9, (N, 1, 1))).astype(np.float32)).astype(BF))
    return d
def setup_inputs_zeros(rng):
    d = setup_inputs(rng); v = d["x"].reshape(N, 128, -1, 4).copy()
    v[np.broadcast_to((rng.random((N, 1, v.shape[2], 1)) < 0.33), v.shape)] = 0
    d["x"] = v.reshape(d["x"].shape)
    return d
def reference(w, x):
    y = np.zeros((N, 128, NC), np.float32)
    for r in range(N):
        for t in range(KT):
            p = mx_ref.matmul(mx_ref.quantize(w[r][:, 512 * t:512 * t + 512]), mx_ref.quantize(x[ROOT][:, 4 * NC * (KT * r + t):4 * NC * (KT * r + t) + 4 * NC]))
            y[r] = p if t == 0 else y[r] + p
    return {"y": y}

@@ -1,0 +1,129 @@
+from concourse.bass import DstId, RemoteDMATransfer
+from concourse.mybir import dt
+
+N = 6
+NC = 128
+TW = 4 * NC
+WORLD = 256
+
+SCRATCH = {
+    "xb": ("sbuf", [128, N * TW], "bfloat16"),
+    "wb": ("sbuf", [128, TW], "bfloat16"),
+    "xq": ("sbuf", [128, N * NC], "float8_e4m3fn_x4"),
+    "xs": ("sbuf", [128, N * NC], "uint8"),
+    "wq": ("sbuf", [128, NC], "float8_e4m3fn_x4"),
+    "ws": ("sbuf", [128, NC], "uint8"),
+    "rq": ("sbuf", [128, NC], "float8_e4m3fn_x4"),
+    "rs": ("sbuf", [128, NC], "uint8"),
+    "ps": ("psum", [128, 512], "float32"),
+    "yb": ("sbuf", [128, NC], "float32"),
+}
+SEMAPHORES = (["ld%d" % r for r in range(N)] + ["q%d" % r for r in range(N)]
+              + ["ldw", "qw", "arr", "sent", "mm", "cp", "st"])
+
+
+def _bits(m):
+    return [1 << i for i in range(m.bit_length()) if (m >> i) & 1]
+
+
+def _shares(bits, n):
+    k = 1
+    while 2 * k * n <= len(bits):
+        k *= 2
+    return [bits[j * k:(j + 1) * k] for j in range(n)]
+
+
+def _plan(T, topo):
+    root = T.cores[T.root]
+    others = [r for r in range(len(T.cores)) if r != T.root]
+    direct = [r for r in others if topo.may_write(root, T.cores[r])]
+    relayed = [r for r in others if r not in direct]
+    idle = [c for c in range(WORLD) if c != root and T.rank_of(c) is None
+            and topo.host(c) == topo.host(root) and topo.chip(c) == topo.chip(root)]
+    ports = [c for c in idle if all(topo.may_write(c, T.cores[r]) for r in relayed)]
+    ports.sort(key=lambda c: topo.die(c) != topo.die(root))
+    leave = _bits(topo.mask(root, T.cores[direct[0]]))
+    stay = [b for b in _bits(topo.mask(root, idle[0])) if b not in leave]
+    calls, carry, expect = [], {}, {r: 0 for r in others}
+    n = len(relayed)
+    for kind, first, engines in (("q", 0, stay), ("s", n, leave)):
+        pieces = []
+        for j, (r, e) in enumerate(zip(relayed, _shares(engines, n))):
+            c = ports[first + j]
+            pieces.append((kind, r, c, e))
+            out = _bits(topo.mask(c, T.cores[r]))
+            carry[c] = (kind, r, len(e), out)
+            expect[r] += len(out)
+        calls.append((relayed if kind == "q" else [], pieces))
+    for i in range(0, len(direct), 2):
+        group = direct[i:i + 2]
+        for kind in ("q", "s"):
+            pieces = [(kind, r, T.cores[r], e) for r, e in zip(group, _shares(leave, len(group)))]
+            for _, r, _, e in pieces:
+                expect[r] += len(e)
+            calls.append((group if kind == "q" else [], pieces))
+    return {"root": root, "order": relayed + direct + [T.root], "calls": calls, "carry": carry, "expect": expect}
+
+
+def _land(T, kind):
+    return T.rq[:].bitcast(dt.uint8) if kind == "q" else T.rs[:]
+
+
+def _piece(T, topo, core, kind, src, dst_core, engines):
+    rid, pid = topo.addr(dst_core, core)
+    return RemoteDMATransfer(dst_ids=[DstId(rid=rid, pnc=pid)], dma_engine_mask=sum(engines), remote_sem=T.sem.arr,
+                             src=src, dst=_land(T, kind))
+
+
+def rank_program(g, core, T, topo):
+    P = _plan(T, topo)
+    rank = T.rank_of(core)
+
+    if core in P["carry"]:
+        kind, r, n_in, out = P["carry"][core]
+        g.wait_ge(T.sem.arr, n_in)
+        g.remote_dma_fused([_piece(T, topo, core, kind, _land(T, kind), T.cores[r], out)], local_sem=T.sem.sent)
+        g.wait_ge(T.sem.sent, len(out))
+        return
+    if rank is None:
+        return
+
+    if core == P["root"]:
+        queues = [g.sync, g.scalar]
+        for i, r in enumerate(P["order"]):
+            queues[i % 2].dma_start(T.xb[:, r * TW:(r + 1) * TW], T.x[:, r * TW:(r + 1) * TW]).then_inc(T.sem["ld%d" % r], 16)
+        queues[len(P["order"]) % 2].dma_start(T.wb[:], T.w[:]).then_inc(T.sem.ldw, 16)
+        for r in P["order"]:
+            if r == rank:
+                g.vector.wait_ge(T.sem.ldw, 16)
+                g.vector.quantize_mx(T.wq[:], T.ws[:], T.wb[:]).then_inc(T.sem.qw, 1)
+            g.vector.wait_ge(T.sem["ld%d" % r], 16)
+            g.vector.quantize_mx(T.xq[:, r * NC:(r + 1) * NC], T.xs[:, r * NC:(r + 1) * NC],
+                                 T.xb[:, r * TW:(r + 1) * TW]).then_inc(T.sem["q%d" % r], 1)
+        left = 0
+        for need, pieces in P["calls"]:
+            for r in need:
+                g.wait_ge(T.sem["q%d" % r], 1)
+            g.remote_dma_fused(
+                [_piece(T, topo, core, kind,
+                        T.xq[:, r * NC:(r + 1) * NC].bitcast(dt.uint8) if kind == "q" else T.xs[:, r * NC:(r + 1) * NC],
+                        c, e) for kind, r, c, e in pieces], local_sem=T.sem.sent)
+            left += sum(len(e) for _, _, _, e in pieces)
+        g.wait_ge(T.sem.sent, left)
+        g.tensor.wait_ge(T.sem.qw, 1)
+        g.tensor.wait_ge(T.sem["q%d" % rank], 1)
+        xq, xs = T.xq[:, rank * NC:(rank + 1) * NC], T.xs[:, rank * NC:(rank + 1) * NC]
+    else:
+        g.sync.dma_start(T.wb[:], T.w[:]).then_inc(T.sem.ldw, 16)
+        g.vector.wait_ge(T.sem.ldw, 16)
+        g.vector.quantize_mx(T.wq[:], T.ws[:], T.wb[:]).then_inc(T.sem.qw, 1)
+        g.tensor.wait_ge(T.sem.qw, 1)
+        g.tensor.wait_ge(T.sem.arr, P["expect"][rank])
+        xq, xs = T.rq[:], T.rs[:]
+
+    g.tensor.matmul_mx(T.ps[:, 0:NC], T.wq[:], T.ws[:], xq, xs, True, True).then_inc(T.sem.mm, 1)
+    g.vector.wait_ge(T.sem.mm, 1)
+    g.vector.tensor_copy(T.yb[:], T.ps[:, 0:NC]).then_inc(T.sem.cp, 1)
+    g.sync.wait_ge(T.sem.cp, 1)
+    g.sync.dma_start(T.y[:], T.yb[:]).then_inc(T.sem.st, 16)
+    g.sync.wait_ge(T.sem.st, 16)

@@ -5,6 +5,7 @@ N = 6
 NC = 128
 TW = 4 * NC
 WORLD = 256
+DIRECT_GROUP = 2
 
 SCRATCH = {
     "xb": ("sbuf", [128, N * TW], "bfloat16"),
@@ -19,7 +20,7 @@ SCRATCH = {
     "yb": ("sbuf", [128, NC], "float32"),
 }
 SEMAPHORES = (["ld%d" % r for r in range(N)] + ["q%d" % r for r in range(N)]
-              + ["ldw", "qw", "arr", "sent", "mm", "cp", "st"])
+              + ["ldw", "qw", "ins", "inq", "arr", "sent", "mm", "cp", "st"])
 
 
 def _bits(m):
@@ -45,22 +46,22 @@ def _plan(T, topo):
     leave = _bits(topo.mask(root, T.cores[direct[0]]))
     stay = [b for b in _bits(topo.mask(root, idle[0])) if b not in leave]
     calls, carry, expect = [], {}, {r: 0 for r in others}
-    n = len(relayed)
-    for kind, first, engines in (("q", 0, stay), ("s", n, leave)):
-        pieces = []
-        for j, (r, e) in enumerate(zip(relayed, _shares(engines, n))):
-            c = ports[first + j]
-            pieces.append((kind, r, c, e))
-            out = _bits(topo.mask(c, T.cores[r]))
-            carry[c] = (kind, r, len(e), out)
-            expect[r] += len(out)
-        calls.append((relayed if kind == "q" else [], pieces))
-    for i in range(0, len(direct), 2):
-        group = direct[i:i + 2]
+
+    def hand(kind, r, c, e):
+        out = _bits(topo.mask(c, T.cores[r]))
+        carry.setdefault(c, []).append((kind, r, len(e), out))
+        expect[r] += len(out)
+        return (kind, r, c, e, "in" + kind)
+
+    for j, r in enumerate(relayed):
+        calls.append(([r], [hand("s", r, ports[j], stay)]))
+    calls.append(([], [hand("q", r, ports[j], e) for j, (r, e) in enumerate(zip(relayed, _shares(stay, len(relayed))))]))
+    for i in range(0, len(direct), DIRECT_GROUP):
+        group = direct[i:i + DIRECT_GROUP]
         for kind in ("q", "s"):
-            pieces = [(kind, r, T.cores[r], e) for r, e in zip(group, _shares(leave, len(group)))]
-            for _, r, _, e in pieces:
-                expect[r] += len(e)
+            pieces = [(kind, r, T.cores[r], e, "arr") for r, e in zip(group, _shares(leave, len(group)))]
+            for p in pieces:
+                expect[p[1]] += len(p[3])
             calls.append((group if kind == "q" else [], pieces))
     return {"root": root, "order": relayed + direct + [T.root], "calls": calls, "carry": carry, "expect": expect}
 
@@ -69,9 +70,9 @@ def _land(T, kind):
     return T.rq[:].bitcast(dt.uint8) if kind == "q" else T.rs[:]
 
 
-def _piece(T, topo, core, kind, src, dst_core, engines):
+def _piece(T, topo, core, kind, src, dst_core, engines, sem):
     rid, pid = topo.addr(dst_core, core)
-    return RemoteDMATransfer(dst_ids=[DstId(rid=rid, pnc=pid)], dma_engine_mask=sum(engines), remote_sem=T.sem.arr,
+    return RemoteDMATransfer(dst_ids=[DstId(rid=rid, pnc=pid)], dma_engine_mask=sum(engines), remote_sem=T.sem[sem],
                              src=src, dst=_land(T, kind))
 
 
@@ -80,10 +81,12 @@ def rank_program(g, core, T, topo):
     rank = T.rank_of(core)
 
     if core in P["carry"]:
-        kind, r, n_in, out = P["carry"][core]
-        g.wait_ge(T.sem.arr, n_in)
-        g.remote_dma_fused([_piece(T, topo, core, kind, _land(T, kind), T.cores[r], out)], local_sem=T.sem.sent)
-        g.wait_ge(T.sem.sent, len(out))
+        left = 0
+        for kind, r, n_in, out in P["carry"][core]:
+            g.wait_ge(T.sem["in" + kind], n_in)
+            g.remote_dma_fused([_piece(T, topo, core, kind, _land(T, kind), T.cores[r], out, "arr")], local_sem=T.sem.sent)
+            left += len(out)
+        g.wait_ge(T.sem.sent, left)
         return
     if rank is None:
         return
@@ -92,7 +95,8 @@ def rank_program(g, core, T, topo):
         queues = [g.sync, g.scalar]
         for i, r in enumerate(P["order"]):
             queues[i % 2].dma_start(T.xb[:, r * TW:(r + 1) * TW], T.x[:, r * TW:(r + 1) * TW]).then_inc(T.sem["ld%d" % r], 16)
-        queues[len(P["order"]) % 2].dma_start(T.wb[:], T.w[:]).then_inc(T.sem.ldw, 16)
+            if r == rank:
+                queues[(i + 1) % 2].dma_start(T.wb[:], T.w[:]).then_inc(T.sem.ldw, 16)
         for r in P["order"]:
             if r == rank:
                 g.vector.wait_ge(T.sem.ldw, 16)
@@ -107,8 +111,8 @@ def rank_program(g, core, T, topo):
             g.remote_dma_fused(
                 [_piece(T, topo, core, kind,
                         T.xq[:, r * NC:(r + 1) * NC].bitcast(dt.uint8) if kind == "q" else T.xs[:, r * NC:(r + 1) * NC],
-                        c, e) for kind, r, c, e in pieces], local_sem=T.sem.sent)
-            left += sum(len(e) for _, _, _, e in pieces)
+                        c, e, sem) for kind, r, c, e, sem in pieces], local_sem=T.sem.sent)
+            left += sum(len(p[3]) for p in pieces)
         g.wait_ge(T.sem.sent, left)
         g.tensor.wait_ge(T.sem.qw, 1)
         g.tensor.wait_ge(T.sem["q%d" % rank], 1)

from concourse.bass import DstId, RemoteDMATransfer
from concourse.mybir import dt

N = 6
NC = 128
TW = 4 * NC
WORLD = 256
DIRECT_GROUP = 2

SCRATCH = {
    "xb": ("sbuf", [128, N * TW], "bfloat16"),
    "wb": ("sbuf", [128, TW], "bfloat16"),
    "xq": ("sbuf", [128, N * NC], "float8_e4m3fn_x4"),
    "xs": ("sbuf", [128, N * NC], "uint8"),
    "wq": ("sbuf", [128, NC], "float8_e4m3fn_x4"),
    "ws": ("sbuf", [128, NC], "uint8"),
    "rq": ("sbuf", [128, NC], "float8_e4m3fn_x4"),
    "rs": ("sbuf", [128, NC], "uint8"),
    "ps": ("psum", [128, 512], "float32"),
    "yb": ("sbuf", [128, NC], "float32"),
}
SEMAPHORES = (["ld%d" % r for r in range(N)] + ["q%d" % r for r in range(N)]
              + ["ldw", "qw", "ins", "inq", "arr", "sent", "mm", "cp", "st"])


def _bits(m):
    return [1 << i for i in range(m.bit_length()) if (m >> i) & 1]


def _shares(bits, n):
    k = 1
    while 2 * k * n <= len(bits):
        k *= 2
    return [bits[j * k:(j + 1) * k] for j in range(n)]


def _plan(T, topo):
    root = T.cores[T.root]
    others = [r for r in range(len(T.cores)) if r != T.root]
    direct = [r for r in others if topo.may_write(root, T.cores[r])]
    relayed = [r for r in others if r not in direct]
    idle = [c for c in range(WORLD) if c != root and T.rank_of(c) is None
            and topo.host(c) == topo.host(root) and topo.chip(c) == topo.chip(root)]
    ports = [c for c in idle if all(topo.may_write(c, T.cores[r]) for r in relayed)]
    ports.sort(key=lambda c: topo.die(c) != topo.die(root))
    leave = _bits(topo.mask(root, T.cores[direct[0]]))
    stay = [b for b in _bits(topo.mask(root, idle[0])) if b not in leave]
    calls, carry, expect = [], {}, {r: 0 for r in others}

    def hand(kind, r, c, e):
        out = _bits(topo.mask(c, T.cores[r]))
        carry.setdefault(c, []).append((kind, r, len(e), out))
        expect[r] += len(out)
        return (kind, r, c, e, "in" + kind)

    for j, r in enumerate(relayed):
        calls.append(([r], [hand("s", r, ports[j], stay)]))
    calls.append(([], [hand("q", r, ports[j], e) for j, (r, e) in enumerate(zip(relayed, _shares(stay, len(relayed))))]))
    for i in range(0, len(direct), DIRECT_GROUP):
        group = direct[i:i + DIRECT_GROUP]
        for kind in ("q", "s"):
            pieces = [(kind, r, T.cores[r], e, "arr") for r, e in zip(group, _shares(leave, len(group)))]
            for p in pieces:
                expect[p[1]] += len(p[3])
            calls.append((group if kind == "q" else [], pieces))
    return {"root": root, "order": relayed + direct + [T.root], "calls": calls, "carry": carry, "expect": expect}


def _land(T, kind):
    return T.rq[:].bitcast(dt.uint8) if kind == "q" else T.rs[:]


def _piece(T, topo, core, kind, src, dst_core, engines, sem):
    rid, pid = topo.addr(dst_core, core)
    return RemoteDMATransfer(dst_ids=[DstId(rid=rid, pnc=pid)], dma_engine_mask=sum(engines), remote_sem=T.sem[sem],
                             src=src, dst=_land(T, kind))


def rank_program(g, core, T, topo):
    P = _plan(T, topo)
    rank = T.rank_of(core)

    if core in P["carry"]:
        left = 0
        for kind, r, n_in, out in P["carry"][core]:
            g.wait_ge(T.sem["in" + kind], n_in)
            g.remote_dma_fused([_piece(T, topo, core, kind, _land(T, kind), T.cores[r], out, "arr")], local_sem=T.sem.sent)
            left += len(out)
        g.wait_ge(T.sem.sent, left)
        return
    if rank is None:
        return

    if core == P["root"]:
        queues = [g.sync, g.scalar]
        for i, r in enumerate(P["order"]):
            queues[i % 2].dma_start(T.xb[:, r * TW:(r + 1) * TW], T.x[:, r * TW:(r + 1) * TW]).then_inc(T.sem["ld%d" % r], 16)
            if r == rank:
                queues[(i + 1) % 2].dma_start(T.wb[:], T.w[:]).then_inc(T.sem.ldw, 16)
        for r in P["order"]:
            if r == rank:
                g.vector.wait_ge(T.sem.ldw, 16)
                g.vector.quantize_mx(T.wq[:], T.ws[:], T.wb[:]).then_inc(T.sem.qw, 1)
            g.vector.wait_ge(T.sem["ld%d" % r], 16)
            g.vector.quantize_mx(T.xq[:, r * NC:(r + 1) * NC], T.xs[:, r * NC:(r + 1) * NC],
                                 T.xb[:, r * TW:(r + 1) * TW]).then_inc(T.sem["q%d" % r], 1)
        left = 0
        for need, pieces in P["calls"]:
            for r in need:
                g.wait_ge(T.sem["q%d" % r], 1)
            g.remote_dma_fused(
                [_piece(T, topo, core, kind,
                        T.xq[:, r * NC:(r + 1) * NC].bitcast(dt.uint8) if kind == "q" else T.xs[:, r * NC:(r + 1) * NC],
                        c, e, sem) for kind, r, c, e, sem in pieces], local_sem=T.sem.sent)
            left += sum(len(p[3]) for p in pieces)
        g.wait_ge(T.sem.sent, left)
        g.tensor.wait_ge(T.sem.qw, 1)
        g.tensor.wait_ge(T.sem["q%d" % rank], 1)
        xq, xs = T.xq[:, rank * NC:(rank + 1) * NC], T.xs[:, rank * NC:(rank + 1) * NC]
    else:
        g.sync.dma_start(T.wb[:], T.w[:]).then_inc(T.sem.ldw, 16)
        g.vector.wait_ge(T.sem.ldw, 16)
        g.vector.quantize_mx(T.wq[:], T.ws[:], T.wb[:]).then_inc(T.sem.qw, 1)
        g.tensor.wait_ge(T.sem.qw, 1)
        g.tensor.wait_ge(T.sem.arr, P["expect"][rank])
        xq, xs = T.rq[:], T.rs[:]

    g.tensor.matmul_mx(T.ps[:, 0:NC], T.wq[:], T.ws[:], xq, xs, True, True).then_inc(T.sem.mm, 1)
    g.vector.wait_ge(T.sem.mm, 1)
    g.vector.tensor_copy(T.yb[:], T.ps[:, 0:NC]).then_inc(T.sem.cp, 1)
    g.sync.wait_ge(T.sem.cp, 1)
    g.sync.dma_start(T.y[:], T.yb[:]).then_inc(T.sem.st, 16)
    g.sync.wait_ge(T.sem.st, 16)
